import numpy as np
import ml_dtypes


def mxq(x, axis, fmt="e4m3"):
    dtype, down = {"e4m3": (ml_dtypes.float8_e4m3fn, 7), "e5m2": (ml_dtypes.float8_e5m2, 14)}[fmt]
    v = np.moveaxis(np.asarray(x, np.float32).astype(ml_dtypes.bfloat16).astype(np.float64), axis, -1)
    blocks = v.reshape(v.shape[:-1] + (-1, 32))
    amax = np.abs(blocks).max(-1, keepdims=True)
    byte = np.maximum(np.where(amax > 0, np.frexp(amax)[1] - 1 + 127, 0) - down, 1)
    scale = np.exp2(byte - 127.0)
    codes = (blocks / scale).astype(np.float32).astype(dtype).astype(np.float64)
    return np.moveaxis((codes * scale).reshape(v.shape), -1, axis)


WIDE = False


def mx_kscale(k):
    if not WIDE:
        return np.ones(k)
    levels = np.array([10, -10, 5, -5, 0])
    if k % 512:
        return np.exp2(np.random.permutation(np.resize(levels, k // 32))).repeat(32)
    a = np.empty((k // 512, 16))
    for p in range(k // 512):
        a[p, :8] = np.random.permutation(np.resize(levels, 8))
        for g in range(8):
            far = levels[np.abs(levels - a[p, g]) >= 10]
            a[p, g + 8] = far[np.random.randint(len(far))]
    return np.exp2(a.ravel()).repeat(32)


def f64(x):
    return np.asarray(x).astype(np.float64)


def striped(idx):
    return np.tile(idx.reshape(-1, 16).T, (8, 1)).astype(np.uint16)


def unstriped(offs):
    return offs[:16].T.reshape(-1).astype(np.int64)

def planes(y):
    n, m = y.shape
    v = y.astype(np.float32).astype(ml_dtypes.bfloat16).astype(np.float64).reshape(n // 32, 32, m)
    top = np.abs(v).max(1)
    byte = np.clip(np.where(top > 0, np.frexp(top)[1] - 1 + 127 - 7, 1), 1, 254)
    codes = (v * np.exp2(127.0 - byte)[:, None, :]).reshape(n, m).astype(np.float32).astype(ml_dtypes.float8_e4m3fn).view(np.uint8)
    words = codes.reshape(n // 512, 128, 4, m).transpose(0, 1, 3, 2)
    return np.ascontiguousarray(words), np.ascontiguousarray(byte.astype(np.uint8).reshape(n // 512, 16, m))


K, T, S, V, H = 512, 1024, 512, 256, 512


def setup_inputs():
    n = np.random.standard_normal
    s = mx_kscale(K)[:, None]
    u = mx_kscale(H)
    return {
        "xT": (n((K, T)) * s).astype(np.float32),
        "w1": (n((K, H)) / np.sqrt(K) / s * u).astype(np.float32),
        "w2": (n((H, H)) / np.sqrt(3 * H) / u[:, None]).astype(np.float32),
        "w3": (n((H, H)) / np.sqrt(3 * H) / u[:, None]).astype(np.float32),
        "w4": (n((H, H)) / np.sqrt(3 * H) / u[:, None]).astype(np.float32),
        "offs": striped(np.random.permutation(T)[:S]),
        "pos1": striped(np.random.permutation(S)[:V]),
        "pos2": striped(np.random.permutation(S)[:V]),
        "pos3": striped(np.random.permutation(S)[:V]),
    }


def reference(xT, w1, w2, w3, w4, offs, pos1, pos2, pos3):
    xq = mxq(f64(xT)[:, unstriped(offs)], 0, "e4m3")
    h = mxq(f64(w1), 0, "e4m3").T @ xq
    g0 = h[:, unstriped(pos1)]
    g1 = h[:, unstriped(pos2)]
    g2 = h[:, unstriped(pos3)]
    z1 = (g0 + g1 + g2) / 3
    z2 = np.maximum(np.maximum(g0, g1), g2)
    z3 = np.minimum(np.minimum(g0, g1), g2)
    out_0 = mxq(f64(w2), 0, "e4m3").T @ mxq(z1, 0, "e4m3") + mxq(f64(w3), 0, "e4m3").T @ mxq(z2, 0, "e4m3") + mxq(f64(w4), 0, "e4m3").T @ mxq(z3, 0, "e4m3")
    return (out_0,) + planes(out_0)

from contextlib import ExitStack

import concourse.mybir as mybir
from concourse.masks import make_identity

K, T, S, V, H = 512, 1024, 512, 256, 512
FLOPS = 2 * K * H * S + 3 * 2 * H * H * V

F32 = mybir.dt.float32
BF16 = mybir.dt.bfloat16
I32 = mybir.dt.int32
U32 = mybir.dt.uint32
U16 = mybir.dt.uint16
U8 = mybir.dt.uint8
FP8X4 = mybir.dt.float8_e4m3fn_x4
ALU = mybir.AluOpType
COPY = mybir.ActivationFunctionType.Copy

P = 128
PACK = 4
D = 3
HALF = V // 2


def tile_picked_pna_none_lo_kernel(
    tc, xT, w1, w2, w3, w4, offs, pos1, pos2, pos3, out_0, out_1, out_2
):
    nc = tc.nc
    with ExitStack() as ctx:
        sb = ctx.enter_context(tc.tile_pool(name="sb", bufs=1))
        ps = ctx.enter_context(tc.psum_pool(name="ps", bufs=1))

        def quantize(codes, scales, values):
            nc.vector.quantize_mx(out=codes.bitcast(FP8X4), scales=scales, in_=values)

        def dealt(w_bf, w_raw):
            dst = w_bf[:].rearrange("p (u e m j) -> p u m j e", u=2, e=2, j=PACK)
            src = w_raw[:].rearrange("p (j m u e) -> p u m j e", j=PACK, u=2, e=2)
            return dst, src

        x_rows = xT.rearrange("(p j) c -> p j c", j=PACK)
        x_raw = [sb.tile([P, T], F32, name="x_raw%d" % j) for j in range(PACK)]
        offs_sb = sb.tile([P, S // 16], U16, name="offs_sb")
        pos_sb = [sb.tile([P, V // 16], U16, name="pos_sb%d" % d) for d in range(D)]
        w_raw = [sb.tile([P, PACK * H], F32, name="w_raw%d" % n) for n in range(4)]
        w_hbm = [w.rearrange("(p j) c -> p (j c)", j=PACK) for w in (w1, w2, w3, w4)]
        nc.sync.dma_start(x_raw[0][:], x_rows[:, 0, :])
        nc.sync.dma_start(offs_sb[:], offs)
        for j in range(1, PACK):
            nc.sync.dma_start(x_raw[j][:], x_rows[:, j, :])
        nc.sync.dma_start(w_raw[0][:], w_hbm[0])
        nc.sync.dma_start(w_raw[1][:], w_hbm[1])
        for d, pos in enumerate((pos1, pos2, pos3)):
            nc.sync.dma_start(pos_sb[d][:], pos)
        nc.sync.dma_start(w_raw[2][:], w_hbm[2])
        nc.sync.dma_start(w_raw[3][:], w_hbm[3])

        ident = sb.tile([P, P], F32, name="ident")
        make_identity(nc, ident[:])

        x_pick = [sb.tile([P, 2, S], F32, name="x_pick%d" % u) for u in range(2)]
        x_bf = sb.tile([P, S * PACK], BF16, name="x_bf", align_bytes=64)
        x_pairs = x_bf[:].rearrange("p (c i u e) -> p u c e i", i=4, u=2, e=2)
        for u in range(2):
            for e in range(2):
                nc.vector.tensor_copy(x_pick[u][:, e, :], x_raw[2 * u + e][:].indirect(offs_sb[:]))
            src = x_pick[u][:].rearrange("p e (c i) -> p c e i", i=4)
            if u == 0:
                nc.scalar.copy(x_pairs[:, u], src)
            else:
                nc.vector.tensor_copy(x_pairs[:, u], src)
        x_codes = sb.tile([P, S], U32, name="x_codes", tag="late", align_bytes=64)
        x_scales = sb.tile([P, S], U8, name="x_scales", align_bytes=64)
        quantize(x_codes[:], x_scales[:], x_bf[:])

        w_codes = [sb.tile([P, H], U32, name="w1_codes", align_bytes=64)]
        w_scales = [sb.tile([P, H], U8, name="w_scales%d" % n, align_bytes=64) for n in range(4)]
        w1_bf = sb.tile([P, PACK * H], BF16, name="w1_bf", align_bytes=64)
        dst, src = dealt(w1_bf, w_raw[0])
        for u in range(2):
            nc.scalar.copy(dst[:, u], src[:, u])

        h_sb = [sb.tile([P, S], F32, name="h_sb%d" % t, tag="h%d" % t, align_bytes=64) for t in range(PACK)]
        h_ps = [ps.tile([P, S], F32, name="h_ps%d" % t, tag="bank%d" % t) for t in range(PACK)]
        for t in range(PACK):
            cols = slice(P * t, P * (t + 1))
            quantize(w_codes[0][:, cols], w_scales[0][:, cols], w1_bf[:, PACK * P * t : PACK * P * (t + 1)])
            nc.tensor.matmul_mx(
                out=h_ps[t][:],
                lhsT=w_codes[0][:, cols].bitcast(FP8X4),
                lhsT_scale=w_scales[0][:, cols],
                rhs=x_codes[:].bitcast(FP8X4),
                rhs_scale=x_scales[:],
                start=True,
                stop=True,
            )
        for t in range(PACK):
            nc.scalar.copy(h_sb[t][:], h_ps[t][:])

        g = [sb.tile([P, D, 2, V], F32, name="g%d" % u) for u in range(2)]
        sum_ps = [ps.tile([P, 2, 2, P], F32, name="sum_ps%d" % u, tag="bank%d" % (4 + u)) for u in range(2)]
        for t in range(PACK):
            u, e = divmod(t, 2)
            for d in range(D):
                nc.vector.tensor_copy(g[u][:, d, e, :], h_sb[t][:].indirect(pos_sb[d][:]))
            for half in range(2):
                for d in range(D):
                    nc.tensor.matmul(
                        sum_ps[u][:, half, e, :],
                        lhsT=g[u][:, d, e, HALF * half : HALF * (half + 1)],
                        rhs=ident[:],
                        is_transpose=True,
                        start=(d == 0),
                        stop=(d == D - 1),
                    )

        late_codes = sb.tile([P, D * H], U32, name="late_codes", tag="h3", align_bytes=64)
        w_codes.extend(late_codes[:, H * n : H * (n + 1)] for n in range(D))
        w2_bf = sb.tile([P, PACK * H], BF16, name="w2_bf", tag="late", align_bytes=64)
        nc.scalar.copy(*dealt(w2_bf, w_raw[1]))
        quantize(w_codes[1], w_scales[1][:], w2_bf[:])
        for n in (2, 3):
            w_bf = sb.tile([P, PACK * H], BF16, name="w_bf%d" % n, align_bytes=64)
            dst = w_bf[:].rearrange("p (t m j) -> p m t j", t=PACK, j=PACK)
            src = w_raw[n][:].rearrange("p (j m t) -> p m t j", j=PACK, t=PACK)
            nc.gpsimd.tensor_scalar(dst, src, 1.0, 0.0, ALU.mult, ALU.add)
            quantize(w_codes[n], w_scales[n][:], w_bf[:])

        g_bf = sb.tile([P, 2, D, V * 2], BF16, name="g_bf")
        mean_t = sb.tile([P, 2, 2, P * 2], BF16, name="mean_t")
        back_ps = ps.tile([P, 2, 2, HALF], F32, name="back_ps", tag="bank6")

        def round_neighbours(u):
            nc.scalar.copy(
                g_bf[:, u].rearrange("p d (c i e) -> p d c e i", i=4, e=2),
                g[u][:].rearrange("p d e (c i) -> p d c e i", i=4),
            )

        def round_mean(u):
            nc.scalar.activation(
                mean_t[:, :, u, :].rearrange("v h (p e) -> v h p e", e=2),
                sum_ps[u][:].rearrange("v h e p -> v h p e"),
                COPY,
                scale=1.0 / D,
            )
            for half in range(2):
                nc.tensor.transpose(back_ps[:, half, u, :], mean_t[:, half, u, :].bitcast(F32), ident[:])

        for u in range(2):
            round_neighbours(u)
            round_mean(u)
        z1_bf = sb.tile([P, V * PACK], BF16, name="z1_bf", align_bytes=64)
        nc.scalar.copy(
            z1_bf[:].bitcast(F32).rearrange("p (h v u) -> p h v u", h=2, u=2),
            back_ps[:].rearrange("p h u v -> p h v u"),
        )

        z_codes = [sb.tile([P, V], U32, name="z_codes%d" % n, align_bytes=64) for n in range(D)]
        z_scales = [sb.tile([P, V], U8, name="z_scales%d" % n, align_bytes=64) for n in range(D)]
        y_codes = sb.tile([P, V], U32, name="y_codes", align_bytes=64)
        y_scales = sb.tile([P, V], U8, name="y_scales", align_bytes=64)
        out_rows = out_0.rearrange("(p t) v -> p t v", t=PACK)
        out_words = out_1.rearrange("z p c r -> (z p) (c r)").bitcast(I32)
        out_scales = out_2.rearrange("z q c -> (z q) c").bitcast(I32)
        y_banks = ((0, 1, 2, 3), (4, 5, 7, 6))

        ops = (ALU.max, ALU.min)
        two = [sb.tile([P, 2, V * 2], BF16, name="two%d" % n) for n in range(2)]
        z2_bf = sb.tile([P, V * PACK], BF16, name="z2_bf", align_bytes=64)
        z3_bf = [sb.tile([P, HALF * PACK], BF16, name="z3_bf%d" % half, align_bytes=64) for half in range(2)]

        def of_three(n, z_bf, cols):
            nc.vector.tensor_tensor(
                z_bf[:].rearrange("p (v u e) -> p v u e", u=2, e=2),
                two[n][:].rearrange("p u (v e) -> p v u e", e=2)[:, cols],
                g_bf[:, :, 2, :].rearrange("p u (v e) -> p v u e", e=2)[:, cols],
                ops[n],
            )

        y_ps = [
            [ps.tile([P, HALF], F32, name="y_ps%d_%d" % (half, t), tag="bank%d" % y_banks[half][t]) for t in range(PACK)]
            for half in range(2)
        ]

        def passes(n, half):
            cols = slice(HALF * half, HALF * (half + 1))
            for t in range(PACK):
                w_cols = slice(P * t, P * (t + 1))
                nc.tensor.matmul_mx(
                    out=y_ps[half][t][:],
                    lhsT=w_codes[1 + n][:, w_cols].bitcast(FP8X4),
                    lhsT_scale=w_scales[1 + n][:, w_cols],
                    rhs=z_codes[n][:, cols].bitcast(FP8X4),
                    rhs_scale=z_scales[n][:, cols],
                    start=(n == 1),
                    stop=(n == 2),
                )

        def hand_out(half):
            cols = slice(HALF * half, HALF * (half + 1))
            y_sb = sb.tile([P, PACK, HALF], F32, name="y_sb%d" % half)
            for t in range(PACK):
                nc.scalar.copy(y_sb[:, t, :], y_ps[half][t][:])
            nc.sync.dma_start(out_rows[:, :, cols], y_sb[:])
            y_bf = sb.tile([P, HALF * PACK], BF16, name="y_bf%d" % half, align_bytes=64)
            dst = y_bf[:].rearrange("p (c i t) -> p c t i", i=4, t=PACK)
            src = y_sb[:].rearrange("p t (c i) -> p c t i", i=4)
            if half == 0:
                nc.scalar.copy(dst, src)
            else:
                nc.vector.tensor_copy(dst, src)
            quantize(y_codes[:, cols], y_scales[:, cols], y_bf[:])
            nc.sync.dma_start(out_words[:, cols], y_codes[:, cols].bitcast(I32))

        halves = [slice(HALF * half, HALF * (half + 1)) for half in range(2)]
        for n in range(2):
            nc.vector.tensor_tensor(two[n][:], g_bf[:, :, 0, :], g_bf[:, :, 1, :], ops[n])
        of_three(0, z2_bf, slice(0, V))
        of_three(1, z3_bf[0], halves[0])
        quantize(z_codes[1][:], z_scales[1][:], z2_bf[:])
        quantize(z_codes[0][:], z_scales[0][:], z1_bf[:])
        quantize(z_codes[2][:, halves[0]], z_scales[2][:, halves[0]], z3_bf[0][:])
        of_three(1, z3_bf[1], halves[1])
        quantize(z_codes[2][:, halves[1]], z_scales[2][:, halves[1]], z3_bf[1][:])
        for n in (1, 0):
            for half in range(2):
                passes(n, half)
        for half in range(2):
            passes(2, half)
            hand_out(half)
        for q in range(4):
            queue = nc.sync if q % 2 == 0 else nc.scalar
            queue.dma_start(out_scales[4 * q : 4 * q + 4, :], y_scales[32 * q : 32 * q + 4, :].bitcast(I32))
